import numpy as np, ml_dtypes
CORES = [12,28,60,100,156,228]
N = 6
S, B = 2, 256
NT = N * S
def setup_inputs(rng):
    a = (rng.standard_normal((128, 128), dtype=np.float32) / 12).astype(ml_dtypes.bfloat16)
    return {"x": rng.standard_normal((N, 128, S * B), dtype=np.float32).astype(ml_dtypes.bfloat16), "a": np.broadcast_to(a, (N, 128, 128)).copy(), "at": np.broadcast_to(a.T, (N, 128, 128)).copy()}
def setup_inputs_big(rng):
    d = setup_inputs(rng)
    for k in ("x",): d[k] = (d[k].astype(np.float32) * 1048576.0).astype(d[k].dtype)
    return d
def setup_inputs_small(rng):
    d = setup_inputs(rng)
    for k in ("x",): d[k] = (d[k].astype(np.float32) * (1 / 1048576.0)).astype(d[k].dtype)
    return d
def setup_inputs_apart(rng):
    d = setup_inputs(rng)
    f = (10.0 ** rng.permutation(np.linspace(-1.5, 1.5, N))).astype(np.float32).reshape(N, 1, 1)
    for k in ("x",): d[k] = (d[k].astype(np.float32) * f).astype(d[k].dtype)
    return d
def reference(x, a, at):
    A = a[0].astype(np.float64); X = [x[t // S][:, B * (t % S):B * (t % S) + B].astype(np.float64) for t in range(NT)]
    f = [None] * NT; b = [None] * NT; h = np.zeros((128, B))
    for t in range(NT):
        h = A.T @ h + X[t]; f[t] = h
    h = np.zeros((128, B))
    for t in range(NT - 1, -1, -1):
        h = A.T @ h + X[t]; b[t] = h
    return {"y": np.stack([np.concatenate([f[r * S + s] + b[r * S + s] for s in range(S)], axis=1) for r in range(N)]).astype(ml_dtypes.bfloat16)}

@@ -1,0 +1,219 @@
+from concourse.bass import DstId, RemoteDMATransfer
+from concourse.mybir import AluOpType
+
+N, B, NSIM = 6, 256, 256
+_POW = {1: 0, 2: 128, 3: 384, 4: 512, 5: 768, 6: 896, 7: 1024, 8: 1152, 9: 1280, 10: 1408}
+_Q2, _Q4 = 256, 640
+
+SCRATCH = {
+    "xs": ("sbuf", [128, 2 * B], "bfloat16"),
+    "x2": ("sbuf", [128, 2 * B], "bfloat16"),
+    "ats": ("sbuf", [128, 128], "bfloat16"),
+    "pw": ("sbuf", [128, 1536], "bfloat16"),
+    "cd": ("sbuf", [128, 2 * B], "bfloat16"),
+    "land": ("sbuf", [128, N * B], "bfloat16"),
+    "ys": ("sbuf", [128, 2 * B], "bfloat16"),
+    "pp0": ("psum", [128, 512], "float32"),
+    "pp1": ("psum", [128, 512], "float32"),
+    "py0": ("psum", [128, 512], "float32"),
+    "py1": ("psum", [128, 512], "float32"),
+    "ps1": ("psum", [128, 512], "float32"),
+    "ps2": ("psum", [128, 512], "float32"),
+    "ps3": ("psum", [128, 512], "float32"),
+}
+SEMAPHORES = ["ld_x", "ld_a", "ld_at", "st0", "st1", "t_p0", "t_p1", "v_p0", "v_p1",
+              "tS1", "tS2", "tS3", "tS4", "vS1", "vS2", "vS3", "vS4", "v_x2", "tY0", "tY1", "vy0", "vy1",
+              "sent"] + ["m%d" % q for q in range(N)]
+
+
+def _mask_of(bits):
+    k = 1
+    while 2 * k <= len(bits):
+        k *= 2
+    return sum(1 << b for b in bits[:k]), k
+
+
+def _bits(masks):
+    both = masks[0]
+    for m in masks[1:]:
+        both &= m
+    return [b for b in range(both.bit_length()) if (both >> b) & 1]
+
+
+def _plan(cores, topo):
+    ranks = range(len(cores))
+    sends, relay, arrive, first = {}, {}, {r: [] for r in ranks}, {}
+    for q in ranks:
+        me = cores[q]
+        kind = lambda r: 0 if r > q else 1
+        direct = [r for r in ranks if r != q and topo.may_write(me, cores[r])]
+        cross = [r for r in ranks if r != q and not topo.may_write(me, cores[r])]
+        load = [(sum(1 for r in cross if kind(r) == p), sum(1 for r in direct if kind(r) == p)) for p in (0, 1)]
+        kinds = sorted([p for p in (0, 1) if load[p] != (0, 0)], key=lambda p: load[p], reverse=True)
+        first[q] = kinds
+        owners = [k for k in range(NSIM) if k != me and topo.host(k) == topo.host(me) and topo.chip(k) == topo.chip(me)
+                  and all(topo.may_write(k, cores[r]) for r in cross)]
+        dies = sorted({topo.die(k) for k in owners})
+        turn = sum(1 for p in ranks if p < q and topo.may_write(cores[p], me))
+        half = (len(cross) + 1) // 2
+        jobs = []
+        for j, part in enumerate((cross[:half], cross[half:])):
+            free = [k for k in owners if topo.die(k) == dies[(turn + j) % len(dies)]]
+            for p in kinds:
+                rs = [r for r in part if kind(r) == p]
+                if rs:
+                    jobs.append((p, free.pop(0), rs))
+        away = _bits([topo.mask(me, cores[r]) for r in direct])
+        home = _bits([topo.mask(me, k) for k in owners])
+        stay = [b for b in home if b not in away]
+        wide = len(direct) < len(jobs)
+        calls = []
+        for i, p in enumerate(kinds):
+            ks = [k for (pp, k, rs) in jobs if pp == p]
+            if ks:
+                m, n = _mask_of(home if (wide and i == 0) else stay)
+                calls.append([(p, m, n, ks)])
+                for (pp, k, rs) in jobs:
+                    if pp == p:
+                        rm, rn = _mask_of(_bits([topo.mask(k, cores[r]) for r in rs]))
+                        relay[k] = (q, n, rm, rn, [cores[r] for r in rs])
+                        for w, r in enumerate(rs):
+                            arrive[r].append((10 + 2 * w + i, abs(r - q), q, rn))
+        slot = 0
+        for i, p in enumerate(kinds):
+            rs = [r for r in direct if kind(r) == p]
+            if rs:
+                m, n = _mask_of(away)
+                calls.append([(p, m, n, [cores[r] for r in rs])])
+                for r in rs:
+                    arrive[r].append((slot + i, abs(r - q), q, n))
+                    slot += 1
+        merged, used = [], 0
+        for call in calls:
+            (p, m, n, ds) = call[0]
+            if merged and merged[-1][-1][0] == p and not (m & ~used) and not any(m & t[1] for t in merged[-1]):
+                merged[-1].append(call[0])
+            else:
+                merged.append(list(call))
+            used |= m
+        sends[q] = merged
+    order = {r: [(q, n) for (_, _, q, n) in sorted(arrive[r])] for r in ranks}
+    return sends, relay, order, first
+
+
+def _issue(g, core, T, topo, q, transfers, src):
+    slot = T.land[:, q * B:(q + 1) * B]
+    sem = T.sem["m%d" % q]
+    if len(transfers) == 1 and len(transfers[0][3]) == 1:
+        (p, m, n, ds) = transfers[0]
+        rid, pid = topo.addr(ds[0], core)
+        g.remote_dma(out_ap=slot, in_ap=src[p], remote_sem=sem, local_sem=T.sem.sent, pid=pid, routing_id=rid,
+                     dma_engine_mask=m)
+        return n
+    trs, total = [], 0
+    for (p, m, n, ds) in transfers:
+        ids = []
+        for d in ds:
+            rid, pid = topo.addr(d, core)
+            ids.append(DstId(rid=rid, pnc=pid))
+        trs.append(RemoteDMATransfer(dst_ids=ids, dma_engine_mask=m, remote_sem=sem, srcs=[src[p]],
+                                     dsts=[slot for _ in ds], alu_op=0))
+        total += n
+    g.remote_dma_fused(trs, local_sem=T.sem.sent)
+    return total
+
+
+def rank_program(g, core, T, topo):
+    cores = list(T.cores)
+    sends, relay, order, first = _plan(cores, topo)
+    S = T.sem
+    r = T.rank_of(core)
+    if r is None:
+        if core in relay:
+            q, fed, m, n, ds = relay[core]
+            g.wait_ge(S["m%d" % q], fed)
+            slot = T.land[:, q * B:(q + 1) * B]
+            g.wait_ge(S.sent, _issue(g, core, T, topo, q, [(0, m, n, ds)], {0: slot}))
+        return
+
+    te, ve = g.tensor, g.vector
+    add = AluOpType.add
+    xh = (T.xs[:, 0:B], T.xs[:, B:2 * B])
+    pp = (T.pp0, T.pp1)
+    pw = T.pw
+    a = pw[:, 0:128]
+    P = lambda k: pw[:, _POW[k]:_POW[k] + 128]
+    kinds = first[r]
+
+    g.sync.dma_start(T.xs[:], T.x[:]).then_inc(S.ld_x, 16)
+    g.scalar.dma_start(a, T.a[:]).then_inc(S.ld_a, 16)
+    g.scalar.dma_start(T.ats[:], T.at[:]).then_inc(S.ld_at, 16)
+
+    te.wait_ge(S.ld_a, 16)
+    te.wait_ge(S.ld_x, 16)
+    ve.wait_ge(S.ld_x, 16)
+    for p in kinds:
+        te.matmul(pp[p][:, 0:B], a, xh[p], True, True).then_inc(S["t_p%d" % p], 1)
+        ve.wait_ge(S["t_p%d" % p], 1)
+        ve.tensor_tensor(T.cd[:, p * B:(p + 1) * B], pp[p][:, 0:B], xh[1 - p], add).then_inc(S["v_p%d" % p], 1)
+
+    src = {p: T.cd[:, p * B:(p + 1) * B] for p in (0, 1)}
+    seen, total = [], 0
+    for call in sends[r]:
+        for t in call:
+            if t[0] not in seen:
+                seen.append(t[0])
+                g.wait_ge(S["v_p%d" % t[0]], 1)
+        total += _issue(g, core, T, topo, r, call, src)
+    g.wait_ge(S.sent, total)
+
+    top = 2 * max(r, N - 1 - r)
+    te.wait_ge(S.ld_at, 16)
+    te.matmul(T.ps1[:, 0:128], T.ats[:], a, True, True).then_inc(S.tS1, 1)
+    te.matmul(T.ps1[:, 128:256], a, T.ats[:], True, True).then_inc(S.tS1, 1)
+    ve.wait_ge(S.tS1, 2)
+    ve.tensor_copy(pw[:, 128:384], T.ps1[:, 0:256]).then_inc(S.vS1, 1)
+    te.matmul(T.py0[:, 0:B], a, xh[1], True, False).then_inc(S.tY0, 1)
+    te.matmul(T.py1[:, 0:B], a, xh[0], True, False).then_inc(S.tY1, 1)
+    te.wait_ge(S.vS1, 1)
+    te.matmul(T.ps2[:, 0:256], pw[:, _Q2:_Q2 + 128], pw[:, 0:256], True, True).then_inc(S.tS2, 1)
+    te.matmul(T.ps2[:, 256:384], P(2), pw[:, _Q2:_Q2 + 128], True, True).then_inc(S.tS2, 1)
+    ve.wait_ge(S.tS2, 2)
+    ve.tensor_copy(pw[:, 384:768], T.ps2[:, 0:384]).then_inc(S.vS2, 1)
+    te.wait_ge(S.vS2, 1)
+    q4 = pw[:, _Q4:_Q4 + 128]
+    w3 = 256 if top <= 6 else 512
+    te.matmul(T.ps3[:, 0:256], q4, pw[:, 0:256], True, True).then_inc(S.tS3, 1)
+    if w3 == 512:
+        te.matmul(T.ps3[:, 256:512], q4, pw[:, 384:640], True, True).then_inc(S.tS3, 1)
+    ve.wait_ge(S.tS3, w3 // 256)
+    ve.tensor_copy(pw[:, 768:768 + w3], T.ps3[:, 0:w3]).then_inc(S.vS3, 1)
+    te.wait_ge(S.vS3, 1)
+    if top > 8:
+        te.matmul(T.ps1[:, 256:512], q4, pw[:, 768:1024], True, True).then_inc(S.tS4, 1)
+        ve.wait_ge(S.tS4, 1)
+        ve.tensor_copy(pw[:, 1280:1536], T.ps1[:, 256:512]).then_inc(S.vS4, 1)
+        te.wait_ge(S.vS4, 1)
+    ve.tensor_tensor(T.x2[:], T.xs[:], T.xs[:], add).then_inc(S.v_x2, 1)
+
+    for i, (q, n) in enumerate(order[r]):
+        last = i == len(order[r]) - 1
+        k = 2 * (abs(r - q) - 1) + 1
+        k0, k1 = (k, k + 1) if q < r else (k + 1, k)
+        blk = T.land[:, q * B:(q + 1) * B]
+        te.wait_ge(S["m%d" % q], n)
+        te.matmul(T.py0[:, 0:B], P(k0), blk, False, last).then_inc(S.tY0, 1)
+        te.matmul(T.py1[:, 0:B], P(k1), blk, False, last).then_inc(S.tY1, 1)
+
+    cnt = 1 + len(order[r])
+    ve.wait_ge(S.v_x2, 1)
+    ve.wait_ge(S.tY0, cnt)
+    ve.tensor_tensor(T.ys[:, 0:B], T.py0[:, 0:B], T.x2[:, 0:B], add).then_inc(S.vy0, 1)
+    ve.wait_ge(S.tY1, cnt)
+    ve.tensor_tensor(T.ys[:, B:2 * B], T.py1[:, 0:B], T.x2[:, B:2 * B], add).then_inc(S.vy1, 1)
+    g.sync.wait_ge(S.vy0, 1)
+    g.sync.dma_start(T.y[:, 0:B], T.ys[:, 0:B]).then_inc(S.st0, 16)
+    g.sync.wait_ge(S.st0, 16)
+    g.scalar.wait_ge(S.vy1, 1)
+    g.scalar.dma_start(T.y[:, B:2 * B], T.ys[:, B:2 * B]).then_inc(S.st1, 16)
+    g.scalar.wait_ge(S.st1, 16)

@@ -12,6 +12,7 @@ SCRATCH = {
     "pw": ("sbuf", [128, 1536], "bfloat16"),
     "cd": ("sbuf", [128, 2 * B], "bfloat16"),
     "land": ("sbuf", [128, N * B], "bfloat16"),
+    "landx": ("sbuf", [128, 2 * B], "bfloat16"),
     "ys": ("sbuf", [128, 2 * B], "bfloat16"),
     "pp0": ("psum", [128, 512], "float32"),
     "pp1": ("psum", [128, 512], "float32"),
@@ -23,13 +24,14 @@ SCRATCH = {
 }
 SEMAPHORES = ["ld_x", "ld_a", "ld_at", "st0", "st1", "t_p0", "t_p1", "v_p0", "v_p1",
               "tS1", "tS2", "tS3", "tS4", "vS1", "vS2", "vS3", "vS4", "v_x2", "tY0", "tY1", "vy0", "vy1",
-              "sent"] + ["m%d" % q for q in range(N)]
+              "sent", "mx"] + ["m%d" % q for q in range(N)]
 
 
-def _mask_of(bits):
+def _mask_of(bits, div=1):
     k = 1
     while 2 * k <= len(bits):
         k *= 2
+    k //= div
     return sum(1 << b for b in bits[:k]), k
 
 
@@ -42,15 +44,14 @@ def _bits(masks):
 
 def _plan(cores, topo):
     ranks = range(len(cores))
-    sends, relay, arrive, first = {}, {}, {r: [] for r in ranks}, {}
+    sends, raw, relay, arrive, first = {}, {}, {}, {r: [] for r in ranks}, {}
     for q in ranks:
         me = cores[q]
         kind = lambda r: 0 if r > q else 1
         direct = [r for r in ranks if r != q and topo.may_write(me, cores[r])]
         cross = [r for r in ranks if r != q and not topo.may_write(me, cores[r])]
         load = [(sum(1 for r in cross if kind(r) == p), sum(1 for r in direct if kind(r) == p)) for p in (0, 1)]
-        kinds = sorted([p for p in (0, 1) if load[p] != (0, 0)], key=lambda p: load[p], reverse=True)
-        first[q] = kinds
+        kinds = sorted((0, 1), key=lambda p: load[p], reverse=True)
         owners = [k for k in range(NSIM) if k != me and topo.host(k) == topo.host(me) and topo.chip(k) == topo.chip(me)
                   and all(topo.may_write(k, cores[r]) for r in cross)]
         dies = sorted({topo.die(k) for k in owners})
@@ -67,6 +68,11 @@ def _plan(cores, topo):
         home = _bits([topo.mask(me, k) for k in owners])
         stay = [b for b in home if b not in away]
         wide = len(direct) < len(jobs)
+        turns = [r for p in kinds for r in direct if kind(r) == p]
+        m, n = _mask_of(away, 1 if wide else 2)
+        raw[q] = (cores[turns[0]], m, n)
+        arrive[turns[0]].append((-1, 0, q, n, True))
+        used = m
         calls = []
         for i, p in enumerate(kinds):
             ks = [k for (pp, k, rs) in jobs if pp == p]
@@ -78,17 +84,15 @@ def _plan(cores, topo):
                         rm, rn = _mask_of(_bits([topo.mask(k, cores[r]) for r in rs]))
                         relay[k] = (q, n, rm, rn, [cores[r] for r in rs])
                         for w, r in enumerate(rs):
-                            arrive[r].append((10 + 2 * w + i, abs(r - q), q, rn))
-        slot = 0
+                            arrive[r].append((10 + 2 * w + i, abs(r - q), q, rn, False))
         for i, p in enumerate(kinds):
-            rs = [r for r in direct if kind(r) == p]
+            rs = [r for r in turns[1:] if kind(r) == p]
             if rs:
                 m, n = _mask_of(away)
                 calls.append([(p, m, n, [cores[r] for r in rs])])
                 for r in rs:
-                    arrive[r].append((slot + i, abs(r - q), q, n))
-                    slot += 1
-        merged, used = [], 0
+                    arrive[r].append((turns.index(r) + i, abs(r - q), q, n, False))
+        merged = []
         for call in calls:
             (p, m, n, ds) = call[0]
             if merged and merged[-1][-1][0] == p and not (m & ~used) and not any(m & t[1] for t in merged[-1]):
@@ -97,8 +101,9 @@ def _plan(cores, topo):
                 merged.append(list(call))
             used |= m
         sends[q] = merged
-    order = {r: [(q, n) for (_, _, q, n) in sorted(arrive[r])] for r in ranks}
-    return sends, relay, order, first
+        first[q] = [p for p in kinds if any(t[0] == p for call in merged for t in call)]
+    order = {r: [(q, n, x) for (_, _, q, n, x) in sorted(arrive[r])] for r in ranks}
+    return sends, raw, relay, order, first
 
 
 def _issue(g, core, T, topo, q, transfers, src):
@@ -125,7 +130,7 @@ def _issue(g, core, T, topo, q, transfers, src):
 
 def rank_program(g, core, T, topo):
     cores = list(T.cores)
-    sends, relay, order, first = _plan(cores, topo)
+    sends, raw, relay, order, first = _plan(cores, topo)
     S = T.sem
     r = T.rank_of(core)
     if r is None:
@@ -157,8 +162,13 @@ def rank_program(g, core, T, topo):
         ve.wait_ge(S["t_p%d" % p], 1)
         ve.tensor_tensor(T.cd[:, p * B:(p + 1) * B], pp[p][:, 0:B], xh[1 - p], add).then_inc(S["v_p%d" % p], 1)
 
+    dst, m, total = raw[r]
+    rid, pid = topo.addr(dst, core)
+    g.wait_ge(S.ld_x, 16)
+    g.remote_dma(out_ap=T.landx[:], in_ap=T.xs[:], remote_sem=S.mx, local_sem=S.sent, pid=pid, routing_id=rid,
+                 dma_engine_mask=m)
     src = {p: T.cd[:, p * B:(p + 1) * B] for p in (0, 1)}
-    seen, total = [], 0
+    seen = []
     for call in sends[r]:
         for t in call:
             if t[0] not in seen:
@@ -196,16 +206,26 @@ def rank_program(g, core, T, topo):
         te.wait_ge(S.vS4, 1)
     ve.tensor_tensor(T.x2[:], T.xs[:], T.xs[:], add).then_inc(S.v_x2, 1)
 
-    for i, (q, n) in enumerate(order[r]):
+    cnt = 1
+    for i, (q, n, isx) in enumerate(order[r]):
         last = i == len(order[r]) - 1
         k = 2 * (abs(r - q) - 1) + 1
         k0, k1 = (k, k + 1) if q < r else (k + 1, k)
-        blk = T.land[:, q * B:(q + 1) * B]
-        te.wait_ge(S["m%d" % q], n)
-        te.matmul(T.py0[:, 0:B], P(k0), blk, False, last).then_inc(S.tY0, 1)
-        te.matmul(T.py1[:, 0:B], P(k1), blk, False, last).then_inc(S.tY1, 1)
+        if isx:
+            up = (1, 0) if q < r else (0, 1)
+            te.wait_ge(S.mx, n)
+            for h in (0, 1):
+                blk = T.landx[:, h * B:(h + 1) * B]
+                te.matmul(T.py0[:, 0:B], P(k0 + up[h]), blk, False, False).then_inc(S.tY0, 1)
+                te.matmul(T.py1[:, 0:B], P(k1 + up[h]), blk, False, False).then_inc(S.tY1, 1)
+            cnt += 2
+        else:
+            blk = T.land[:, q * B:(q + 1) * B]
+            te.wait_ge(S["m%d" % q], n)
+            te.matmul(T.py0[:, 0:B], P(k0), blk, False, last).then_inc(S.tY0, 1)
+            te.matmul(T.py1[:, 0:B], P(k1), blk, False, last).then_inc(S.tY1, 1)
+            cnt += 1
 
-    cnt = 1 + len(order[r])
     ve.wait_ge(S.v_x2, 1)
     ve.wait_ge(S.tY0, cnt)
     ve.tensor_tensor(T.ys[:, 0:B], T.py0[:, 0:B], T.x2[:, 0:B], add).then_inc(S.vy0, 1)

@@ -1,7 +1,7 @@
 from concourse.bass import DstId, RemoteDMATransfer
 from concourse.mybir import AluOpType
 
-N, B, NSIM = 6, 256, 256
+N, B, H, NSIM = 6, 256, 128, 256
 _POW = {1: 0, 2: 128, 3: 384, 4: 512, 5: 768, 6: 896, 7: 1024, 8: 1152, 9: 1280, 10: 1408}
 _Q2, _Q4 = 256, 640
 
@@ -22,9 +22,9 @@ SCRATCH = {
     "ps2": ("psum", [128, 512], "float32"),
     "ps3": ("psum", [128, 512], "float32"),
 }
-SEMAPHORES = ["ld_x", "ld_a", "ld_at", "st0", "st1", "t_p0", "t_p1", "v_p0", "v_p1",
-              "tS1", "tS2", "tS3", "tS4", "vS1", "vS2", "vS3", "vS4", "v_x2", "tY0", "tY1", "vy0", "vy1",
-              "sent", "mx"] + ["m%d" % q for q in range(N)]
+SEMAPHORES = ["ld_x0", "ld_x1", "ld_a", "ld_at", "st0", "st1", "t_p0", "t_p1", "v_p0", "v_p1",
+              "tS1", "tS2", "tS3", "tS4", "vS1", "vS2", "vS3", "vS4", "v_x2", "tY0", "tY0b", "tY1", "vy0", "vy1",
+              "sent", "mxa", "mxb"] + ["m%d" % q for q in range(N)]
 
 
 def _mask_of(bits, div=1):
@@ -64,14 +64,18 @@ def _plan(cores, topo):
                 rs = [r for r in part if kind(r) == p]
                 if rs:
                     jobs.append((p, free.pop(0), rs))
+        if ((turn + 1) // 2) % 2:
+            jobs.reverse()
         away = _bits([topo.mask(me, cores[r]) for r in direct])
         home = _bits([topo.mask(me, k) for k in owners])
         stay = [b for b in home if b not in away]
         wide = len(direct) < len(jobs)
         turns = [r for p in kinds for r in direct if kind(r) == p]
         m, n = _mask_of(away, 1 if wide else 2)
-        raw[q] = (cores[turns[0]], m, n)
-        arrive[turns[0]].append((-1, 0, q, n, True))
+        m2, n2 = _mask_of(away)
+        raw[q] = (cores[turns[0]], kinds[0], m, n, m2, n2)
+        arrive[turns[0]].append((-1, 0, q, n, ("mxa", kinds[0])))
+        arrive[turns[0]].append((0, 0, q, n2, ("mxb", 1 - kinds[0])))
         used = m
         calls = []
         for i, p in enumerate(kinds):
@@ -84,14 +88,14 @@ def _plan(cores, topo):
                         rm, rn = _mask_of(_bits([topo.mask(k, cores[r]) for r in rs]))
                         relay[k] = (q, n, rm, rn, [cores[r] for r in rs])
                         for w, r in enumerate(rs):
-                            arrive[r].append((10 + 2 * w + i, abs(r - q), q, rn, False))
+                            arrive[r].append((10 + 2 * w + 2 * i + ks.index(k), abs(r - q), q, rn, None))
         for i, p in enumerate(kinds):
             rs = [r for r in turns[1:] if kind(r) == p]
             if rs:
                 m, n = _mask_of(away)
                 calls.append([(p, m, n, [cores[r] for r in rs])])
                 for r in rs:
-                    arrive[r].append((turns.index(r) + i, abs(r - q), q, n, False))
+                    arrive[r].append((turns.index(r) + i, abs(r - q), q, n, None))
         merged = []
         for call in calls:
             (p, m, n, ds) = call[0]
@@ -102,7 +106,7 @@ def _plan(cores, topo):
             used |= m
         sends[q] = merged
         first[q] = [p for p in kinds if any(t[0] == p for call in merged for t in call)]
-    order = {r: [(q, n, x) for (_, _, q, n, x) in sorted(arrive[r])] for r in ranks}
+    order = {r: [(q, n, x) for (_, _, q, n, x) in sorted(arrive[r], key=lambda t: t[:3])] for r in ranks}
     return sends, raw, relay, order, first
 
 
@@ -144,32 +148,46 @@ def rank_program(g, core, T, topo):
     te, ve = g.tensor, g.vector
     add = AluOpType.add
     xh = (T.xs[:, 0:B], T.xs[:, B:2 * B])
+    ldx = (S.ld_x0, S.ld_x1)
     pp = (T.pp0, T.pp1)
     pw = T.pw
     a = pw[:, 0:128]
     P = lambda k: pw[:, _POW[k]:_POW[k] + 128]
     kinds = first[r]
+    dst, hf, m1, n1, m2, n2 = raw[r]
 
-    g.sync.dma_start(T.xs[:], T.x[:]).then_inc(S.ld_x, 16)
+    for h in (hf, 1 - hf):
+        g.sync.dma_start(xh[h], T.x[:, h * B:(h + 1) * B]).then_inc(ldx[h], 16)
     g.scalar.dma_start(a, T.a[:]).then_inc(S.ld_a, 16)
     g.scalar.dma_start(T.ats[:], T.at[:]).then_inc(S.ld_at, 16)
 
     te.wait_ge(S.ld_a, 16)
-    te.wait_ge(S.ld_x, 16)
-    ve.wait_ge(S.ld_x, 16)
-    for p in kinds:
+    te.wait_ge(ldx[hf], 16)
+    ve.wait_ge(ldx[1 - hf], 16)
+    for i, p in enumerate(kinds):
         te.matmul(pp[p][:, 0:B], a, xh[p], True, True).then_inc(S["t_p%d" % p], 1)
         ve.wait_ge(S["t_p%d" % p], 1)
         ve.tensor_tensor(T.cd[:, p * B:(p + 1) * B], pp[p][:, 0:B], xh[1 - p], add).then_inc(S["v_p%d" % p], 1)
+        if i == 0:
+            te.wait_ge(ldx[1 - hf], 16)
+            ve.wait_ge(ldx[hf], 16)
 
-    dst, m, total = raw[r]
     rid, pid = topo.addr(dst, core)
-    g.wait_ge(S.ld_x, 16)
-    g.remote_dma(out_ap=T.landx[:], in_ap=T.xs[:], remote_sem=S.mx, local_sem=S.sent, pid=pid, routing_id=rid,
-                 dma_engine_mask=m)
+    g.wait_ge(ldx[hf], 16)
+    g.remote_dma(out_ap=T.landx[:, hf * B:(hf + 1) * B], in_ap=xh[hf], remote_sem=S.mxa, local_sem=S.sent, pid=pid,
+                 routing_id=rid, dma_engine_mask=m1)
+    total = n1
     src = {p: T.cd[:, p * B:(p + 1) * B] for p in (0, 1)}
     seen = []
-    for call in sends[r]:
+    for call in sends[r] + [None]:
+        if n2 and (call is None or call[0][3][0] in cores):
+            g.wait_ge(ldx[1 - hf], 16)
+            g.remote_dma(out_ap=T.landx[:, (1 - hf) * B:(2 - hf) * B], in_ap=xh[1 - hf], remote_sem=S.mxb,
+                         local_sem=S.sent, pid=pid, routing_id=rid, dma_engine_mask=m2)
+            total += n2
+            n2 = 0
+        if call is None:
+            break
         for t in call:
             if t[0] not in seen:
                 seen.append(t[0])
@@ -183,7 +201,10 @@ def rank_program(g, core, T, topo):
     te.matmul(T.ps1[:, 128:256], a, T.ats[:], True, True).then_inc(S.tS1, 1)
     ve.wait_ge(S.tS1, 2)
     ve.tensor_copy(pw[:, 128:384], T.ps1[:, 0:256]).then_inc(S.vS1, 1)
-    te.matmul(T.py0[:, 0:B], a, xh[1], True, False).then_inc(S.tY0, 1)
+    te.wait_ge(S["v_p%d" % kinds[0]], 1)
+    y0 = ((T.py0[:, 0:H], S.tY0), (pp[kinds[0]][:, 0:H], S.tY0b))
+    for j, (bank, ysem) in enumerate(y0):
+        te.matmul(bank, a, T.xs[:, B + j * H:B + (j + 1) * H], True, False).then_inc(ysem, 1)
     te.matmul(T.py1[:, 0:B], a, xh[0], True, False).then_inc(S.tY1, 1)
     te.wait_ge(S.vS1, 1)
     te.matmul(T.ps2[:, 0:256], pw[:, _Q2:_Q2 + 128], pw[:, 0:256], True, True).then_inc(S.tS2, 1)
@@ -206,32 +227,28 @@ def rank_program(g, core, T, topo):
         te.wait_ge(S.vS4, 1)
     ve.tensor_tensor(T.x2[:], T.xs[:], T.xs[:], add).then_inc(S.v_x2, 1)
 
-    cnt = 1
-    for i, (q, n, isx) in enumerate(order[r]):
+    for i, (q, n, half) in enumerate(order[r]):
         last = i == len(order[r]) - 1
         k = 2 * (abs(r - q) - 1) + 1
         k0, k1 = (k, k + 1) if q < r else (k + 1, k)
-        if isx:
-            up = (1, 0) if q < r else (0, 1)
-            te.wait_ge(S.mx, n)
-            for h in (0, 1):
-                blk = T.landx[:, h * B:(h + 1) * B]
-                te.matmul(T.py0[:, 0:B], P(k0 + up[h]), blk, False, False).then_inc(S.tY0, 1)
-                te.matmul(T.py1[:, 0:B], P(k1 + up[h]), blk, False, False).then_inc(S.tY1, 1)
-            cnt += 2
+        if half:
+            up = ((1, 0) if q < r else (0, 1))[half[1]]
+            sem, buf, off = S[half[0]], T.landx, half[1] * B
         else:
-            blk = T.land[:, q * B:(q + 1) * B]
-            te.wait_ge(S["m%d" % q], n)
-            te.matmul(T.py0[:, 0:B], P(k0), blk, False, last).then_inc(S.tY0, 1)
-            te.matmul(T.py1[:, 0:B], P(k1), blk, False, last).then_inc(S.tY1, 1)
-            cnt += 1
+            up, sem, buf, off = 0, S["m%d" % q], T.land, q * B
+        te.wait_ge(sem, n)
+        for j, (bank, ysem) in enumerate(y0):
+            te.matmul(bank, P(k0 + up), buf[:, off + j * H:off + (j + 1) * H], False, last).then_inc(ysem, 1)
+        te.matmul(T.py1[:, 0:B], P(k1 + up), buf[:, off:off + B], False, last).then_inc(S.tY1, 1)
 
+    cnt = 1 + len(order[r])
     ve.wait_ge(S.v_x2, 1)
-    ve.wait_ge(S.tY0, cnt)
-    ve.tensor_tensor(T.ys[:, 0:B], T.py0[:, 0:B], T.x2[:, 0:B], add).then_inc(S.vy0, 1)
+    for j, (bank, ysem) in enumerate(y0):
+        ve.wait_ge(ysem, cnt)
+        ve.tensor_tensor(T.ys[:, j * H:(j + 1) * H], bank, T.x2[:, j * H:(j + 1) * H], add).then_inc(S.vy0, 1)
     ve.wait_ge(S.tY1, cnt)
     ve.tensor_tensor(T.ys[:, B:2 * B], T.py1[:, 0:B], T.x2[:, B:2 * B], add).then_inc(S.vy1, 1)
-    g.sync.wait_ge(S.vy0, 1)
+    g.sync.wait_ge(S.vy0, 2)
     g.sync.dma_start(T.y[:, 0:B], T.ys[:, 0:B]).then_inc(S.st0, 16)
     g.sync.wait_ge(S.st0, 16)
     g.scalar.wait_ge(S.vy1, 1)

from concourse.bass import DstId, RemoteDMATransfer
from concourse.mybir import AluOpType

N, B, H, NSIM = 6, 256, 128, 256
_POW = {1: 0, 2: 128, 3: 384, 4: 512, 5: 768, 6: 896, 7: 1024, 8: 1152, 9: 1280, 10: 1408}
_Q2, _Q4 = 256, 640

SCRATCH = {
    "xs": ("sbuf", [128, 2 * B], "bfloat16"),
    "x2": ("sbuf", [128, 2 * B], "bfloat16"),
    "ats": ("sbuf", [128, 128], "bfloat16"),
    "pw": ("sbuf", [128, 1536], "bfloat16"),
    "cd": ("sbuf", [128, 2 * B], "bfloat16"),
    "land": ("sbuf", [128, N * B], "bfloat16"),
    "landx": ("sbuf", [128, 2 * B], "bfloat16"),
    "ys": ("sbuf", [128, 2 * B], "bfloat16"),
    "pp0": ("psum", [128, 512], "float32"),
    "pp1": ("psum", [128, 512], "float32"),
    "py0": ("psum", [128, 512], "float32"),
    "py1": ("psum", [128, 512], "float32"),
    "ps1": ("psum", [128, 512], "float32"),
    "ps2": ("psum", [128, 512], "float32"),
    "ps3": ("psum", [128, 512], "float32"),
}
SEMAPHORES = ["ld_x0", "ld_x1", "ld_a", "ld_at", "st0", "st1", "t_p0", "t_p1", "v_p0", "v_p1",
              "tS1", "tS2", "tS3", "tS4", "vS1", "vS2", "vS3", "vS4", "v_x2", "tY0", "tY0b", "tY1", "vy0", "vy1",
              "sent", "mxa", "mxb"] + ["m%d" % q for q in range(N)]


def _mask_of(bits, div=1):
    k = 1
    while 2 * k <= len(bits):
        k *= 2
    k //= div
    return sum(1 << b for b in bits[:k]), k


def _bits(masks):
    both = masks[0]
    for m in masks[1:]:
        both &= m
    return [b for b in range(both.bit_length()) if (both >> b) & 1]


def _plan(cores, topo):
    ranks = range(len(cores))
    sends, raw, relay, arrive, first = {}, {}, {}, {r: [] for r in ranks}, {}
    for q in ranks:
        me = cores[q]
        kind = lambda r: 0 if r > q else 1
        direct = [r for r in ranks if r != q and topo.may_write(me, cores[r])]
        cross = [r for r in ranks if r != q and not topo.may_write(me, cores[r])]
        load = [(sum(1 for r in cross if kind(r) == p), sum(1 for r in direct if kind(r) == p)) for p in (0, 1)]
        kinds = sorted((0, 1), key=lambda p: load[p], reverse=True)
        owners = [k for k in range(NSIM) if k != me and topo.host(k) == topo.host(me) and topo.chip(k) == topo.chip(me)
                  and all(topo.may_write(k, cores[r]) for r in cross)]
        dies = sorted({topo.die(k) for k in owners})
        turn = sum(1 for p in ranks if p < q and topo.may_write(cores[p], me))
        half = (len(cross) + 1) // 2
        jobs = []
        for j, part in enumerate((cross[:half], cross[half:])):
            free = [k for k in owners if topo.die(k) == dies[(turn + j) % len(dies)]]
            for p in kinds:
                rs = [r for r in part if kind(r) == p]
                if rs:
                    jobs.append((p, free.pop(0), rs))
        if ((turn + 1) // 2) % 2:
            jobs.reverse()
        away = _bits([topo.mask(me, cores[r]) for r in direct])
        home = _bits([topo.mask(me, k) for k in owners])
        stay = [b for b in home if b not in away]
        wide = len(direct) < len(jobs)
        turns = [r for p in kinds for r in direct if kind(r) == p]
        m, n = _mask_of(away, 1 if wide else 2)
        m2, n2 = _mask_of(away)
        raw[q] = (cores[turns[0]], kinds[0], m, n, m2, n2)
        arrive[turns[0]].append((-1, 0, q, n, ("mxa", kinds[0])))
        arrive[turns[0]].append((0, 0, q, n2, ("mxb", 1 - kinds[0])))
        used = m
        calls = []
        for i, p in enumerate(kinds):
            ks = [k for (pp, k, rs) in jobs if pp == p]
            if ks:
                m, n = _mask_of(home if (wide and i == 0) else stay)
                calls.append([(p, m, n, ks)])
                for (pp, k, rs) in jobs:
                    if pp == p:
                        rm, rn = _mask_of(_bits([topo.mask(k, cores[r]) for r in rs]))
                        relay[k] = (q, n, rm, rn, [cores[r] for r in rs])
                        for w, r in enumerate(rs):
                            arrive[r].append((10 + 2 * w + 2 * i + ks.index(k), abs(r - q), q, rn, None))
        for i, p in enumerate(kinds):
            rs = [r for r in turns[1:] if kind(r) == p]
            if rs:
                m, n = _mask_of(away)
                calls.append([(p, m, n, [cores[r] for r in rs])])
                for r in rs:
                    arrive[r].append((turns.index(r) + i, abs(r - q), q, n, None))
        merged = []
        for call in calls:
            (p, m, n, ds) = call[0]
            if merged and merged[-1][-1][0] == p and not (m & ~used) and not any(m & t[1] for t in merged[-1]):
                merged[-1].append(call[0])
            else:
                merged.append(list(call))
            used |= m
        sends[q] = merged
        first[q] = [p for p in kinds if any(t[0] == p for call in merged for t in call)]
    order = {r: [(q, n, x) for (_, _, q, n, x) in sorted(arrive[r], key=lambda t: t[:3])] for r in ranks}
    return sends, raw, relay, order, first


def _issue(g, core, T, topo, q, transfers, src):
    slot = T.land[:, q * B:(q + 1) * B]
    sem = T.sem["m%d" % q]
    if len(transfers) == 1 and len(transfers[0][3]) == 1:
        (p, m, n, ds) = transfers[0]
        rid, pid = topo.addr(ds[0], core)
        g.remote_dma(out_ap=slot, in_ap=src[p], remote_sem=sem, local_sem=T.sem.sent, pid=pid, routing_id=rid,
                     dma_engine_mask=m)
        return n
    trs, total = [], 0
    for (p, m, n, ds) in transfers:
        ids = []
        for d in ds:
            rid, pid = topo.addr(d, core)
            ids.append(DstId(rid=rid, pnc=pid))
        trs.append(RemoteDMATransfer(dst_ids=ids, dma_engine_mask=m, remote_sem=sem, srcs=[src[p]],
                                     dsts=[slot for _ in ds], alu_op=0))
        total += n
    g.remote_dma_fused(trs, local_sem=T.sem.sent)
    return total


def rank_program(g, core, T, topo):
    cores = list(T.cores)
    sends, raw, relay, order, first = _plan(cores, topo)
    S = T.sem
    r = T.rank_of(core)
    if r is None:
        if core in relay:
            q, fed, m, n, ds = relay[core]
            g.wait_ge(S["m%d" % q], fed)
            slot = T.land[:, q * B:(q + 1) * B]
            g.wait_ge(S.sent, _issue(g, core, T, topo, q, [(0, m, n, ds)], {0: slot}))
        return

    te, ve = g.tensor, g.vector
    add = AluOpType.add
    xh = (T.xs[:, 0:B], T.xs[:, B:2 * B])
    ldx = (S.ld_x0, S.ld_x1)
    pp = (T.pp0, T.pp1)
    pw = T.pw
    a = pw[:, 0:128]
    P = lambda k: pw[:, _POW[k]:_POW[k] + 128]
    kinds = first[r]
    dst, hf, m1, n1, m2, n2 = raw[r]

    for h in (hf, 1 - hf):
        g.sync.dma_start(xh[h], T.x[:, h * B:(h + 1) * B]).then_inc(ldx[h], 16)
    g.scalar.dma_start(a, T.a[:]).then_inc(S.ld_a, 16)
    g.scalar.dma_start(T.ats[:], T.at[:]).then_inc(S.ld_at, 16)

    te.wait_ge(S.ld_a, 16)
    te.wait_ge(ldx[hf], 16)
    ve.wait_ge(ldx[1 - hf], 16)
    for i, p in enumerate(kinds):
        te.matmul(pp[p][:, 0:B], a, xh[p], True, True).then_inc(S["t_p%d" % p], 1)
        ve.wait_ge(S["t_p%d" % p], 1)
        ve.tensor_tensor(T.cd[:, p * B:(p + 1) * B], pp[p][:, 0:B], xh[1 - p], add).then_inc(S["v_p%d" % p], 1)
        if i == 0:
            te.wait_ge(ldx[1 - hf], 16)
            ve.wait_ge(ldx[hf], 16)

    rid, pid = topo.addr(dst, core)
    g.wait_ge(ldx[hf], 16)
    g.remote_dma(out_ap=T.landx[:, hf * B:(hf + 1) * B], in_ap=xh[hf], remote_sem=S.mxa, local_sem=S.sent, pid=pid,
                 routing_id=rid, dma_engine_mask=m1)
    total = n1
    src = {p: T.cd[:, p * B:(p + 1) * B] for p in (0, 1)}
    seen = []
    for call in sends[r] + [None]:
        if n2 and (call is None or call[0][3][0] in cores):
            g.wait_ge(ldx[1 - hf], 16)
            g.remote_dma(out_ap=T.landx[:, (1 - hf) * B:(2 - hf) * B], in_ap=xh[1 - hf], remote_sem=S.mxb,
                         local_sem=S.sent, pid=pid, routing_id=rid, dma_engine_mask=m2)
            total += n2
            n2 = 0
        if call is None:
            break
        for t in call:
            if t[0] not in seen:
                seen.append(t[0])
                g.wait_ge(S["v_p%d" % t[0]], 1)
        total += _issue(g, core, T, topo, r, call, src)
    g.wait_ge(S.sent, total)

    top = 2 * max(r, N - 1 - r)
    te.wait_ge(S.ld_at, 16)
    te.matmul(T.ps1[:, 0:128], T.ats[:], a, True, True).then_inc(S.tS1, 1)
    te.matmul(T.ps1[:, 128:256], a, T.ats[:], True, True).then_inc(S.tS1, 1)
    ve.wait_ge(S.tS1, 2)
    ve.tensor_copy(pw[:, 128:384], T.ps1[:, 0:256]).then_inc(S.vS1, 1)
    te.wait_ge(S["v_p%d" % kinds[0]], 1)
    y0 = ((T.py0[:, 0:H], S.tY0), (pp[kinds[0]][:, 0:H], S.tY0b))
    for j, (bank, ysem) in enumerate(y0):
        te.matmul(bank, a, T.xs[:, B + j * H:B + (j + 1) * H], True, False).then_inc(ysem, 1)
    te.matmul(T.py1[:, 0:B], a, xh[0], True, False).then_inc(S.tY1, 1)
    te.wait_ge(S.vS1, 1)
    te.matmul(T.ps2[:, 0:256], pw[:, _Q2:_Q2 + 128], pw[:, 0:256], True, True).then_inc(S.tS2, 1)
    te.matmul(T.ps2[:, 256:384], P(2), pw[:, _Q2:_Q2 + 128], True, True).then_inc(S.tS2, 1)
    ve.wait_ge(S.tS2, 2)
    ve.tensor_copy(pw[:, 384:768], T.ps2[:, 0:384]).then_inc(S.vS2, 1)
    te.wait_ge(S.vS2, 1)
    q4 = pw[:, _Q4:_Q4 + 128]
    w3 = 256 if top <= 6 else 512
    te.matmul(T.ps3[:, 0:256], q4, pw[:, 0:256], True, True).then_inc(S.tS3, 1)
    if w3 == 512:
        te.matmul(T.ps3[:, 256:512], q4, pw[:, 384:640], True, True).then_inc(S.tS3, 1)
    ve.wait_ge(S.tS3, w3 // 256)
    ve.tensor_copy(pw[:, 768:768 + w3], T.ps3[:, 0:w3]).then_inc(S.vS3, 1)
    te.wait_ge(S.vS3, 1)
    if top > 8:
        te.matmul(T.ps1[:, 256:512], q4, pw[:, 768:1024], True, True).then_inc(S.tS4, 1)
        ve.wait_ge(S.tS4, 1)
        ve.tensor_copy(pw[:, 1280:1536], T.ps1[:, 256:512]).then_inc(S.vS4, 1)
        te.wait_ge(S.vS4, 1)
    ve.tensor_tensor(T.x2[:], T.xs[:], T.xs[:], add).then_inc(S.v_x2, 1)

    for i, (q, n, half) in enumerate(order[r]):
        last = i == len(order[r]) - 1
        k = 2 * (abs(r - q) - 1) + 1
        k0, k1 = (k, k + 1) if q < r else (k + 1, k)
        if half:
            up = ((1, 0) if q < r else (0, 1))[half[1]]
            sem, buf, off = S[half[0]], T.landx, half[1] * B
        else:
            up, sem, buf, off = 0, S["m%d" % q], T.land, q * B
        te.wait_ge(sem, n)
        for j, (bank, ysem) in enumerate(y0):
            te.matmul(bank, P(k0 + up), buf[:, off + j * H:off + (j + 1) * H], False, last).then_inc(ysem, 1)
        te.matmul(T.py1[:, 0:B], P(k1 + up), buf[:, off:off + B], False, last).then_inc(S.tY1, 1)

    cnt = 1 + len(order[r])
    ve.wait_ge(S.v_x2, 1)
    for j, (bank, ysem) in enumerate(y0):
        ve.wait_ge(ysem, cnt)
        ve.tensor_tensor(T.ys[:, j * H:(j + 1) * H], bank, T.x2[:, j * H:(j + 1) * H], add).then_inc(S.vy0, 1)
    ve.wait_ge(S.tY1, cnt)
    ve.tensor_tensor(T.ys[:, B:2 * B], T.py1[:, 0:B], T.x2[:, B:2 * B], add).then_inc(S.vy1, 1)
    g.sync.wait_ge(S.vy0, 2)
    g.sync.dma_start(T.y[:, 0:B], T.ys[:, 0:B]).then_inc(S.st0, 16)
    g.sync.wait_ge(S.st0, 16)
    g.scalar.wait_ge(S.vy1, 1)
    g.scalar.dma_start(T.y[:, B:2 * B], T.ys[:, B:2 * B]).then_inc(S.st1, 16)
    g.scalar.wait_ge(S.st1, 16)
